import numpy as np
import ml_dtypes


def mxq(x, axis, fmt="e4m3"):
    dtype, down = {"e4m3": (ml_dtypes.float8_e4m3fn, 7), "e5m2": (ml_dtypes.float8_e5m2, 14)}[fmt]
    v = np.moveaxis(np.asarray(x, np.float32).astype(ml_dtypes.bfloat16).astype(np.float64), axis, -1)
    blocks = v.reshape(v.shape[:-1] + (-1, 32))
    amax = np.abs(blocks).max(-1, keepdims=True)
    byte = np.maximum(np.where(amax > 0, np.frexp(amax)[1] - 1 + 127, 0) - down, 1)
    scale = np.exp2(byte - 127.0)
    codes = (blocks / scale).astype(np.float32).astype(dtype).astype(np.float64)
    return np.moveaxis((codes * scale).reshape(v.shape), -1, axis)


WIDE = False


def mx_kscale(k):
    if not WIDE:
        return np.ones(k)
    levels = np.array([10, -10, 5, -5, 0])
    if k % 512:
        return np.exp2(np.random.permutation(np.resize(levels, k // 32))).repeat(32)
    a = np.empty((k // 512, 16))
    for p in range(k // 512):
        a[p, :8] = np.random.permutation(np.resize(levels, 8))
        for g in range(8):
            far = levels[np.abs(levels - a[p, g]) >= 10]
            a[p, g + 8] = far[np.random.randint(len(far))]
    return np.exp2(a.ravel()).repeat(32)


BF16 = ml_dtypes.bfloat16


def bf(x):
    return np.asarray(x, np.float32).astype(BF16)


def f64(x):
    return np.asarray(x).astype(np.float64)


E2M1 = np.array([0.0, 0.5, 1.0, 1.5, 2.0, 3.0, 4.0, 6.0, -0.0, -0.5, -1.0, -1.5, -2.0, -3.0, -4.0, -6.0])


def pack_weight(w, fmt):
    k, n = w.shape
    w = f64(bf(w)).reshape(k // 32, 32, n)
    amax = np.abs(w).max(1)
    if fmt == "e4m3":
        byte = np.frexp(amax)[1] - 1 + 127 - 7
    else:
        mant, ex = np.frexp(amax / 6.0)
        byte = np.where(mant > 0.5, ex, ex - 1) + 127
    byte = np.clip(np.where(amax > 0, byte, 1), 1, 254)
    scaled = (w * np.exp2(127.0 - byte)[:, None, :]).reshape(k, n).astype(np.float32)
    by_word = np.ascontiguousarray(scaled.reshape(k // 512, 128, 4, n).transpose(0, 1, 3, 2))
    if fmt == "e4m3":
        words = by_word.astype(ml_dtypes.float8_e4m3fn).view(np.uint8)
    else:
        c = by_word.astype(ml_dtypes.float4_e2m1fn).view(np.uint8) & 0xF
        words = c[..., 0::2] | (c[..., 1::2] << 4)
    return np.ascontiguousarray(words), np.ascontiguousarray(byte.astype(np.uint8).reshape(k // 512, 16, n))


def unpack_weight(words, scales, fmt):
    g, p, n, _ = words.shape
    if fmt == "e4m3":
        vals = np.ascontiguousarray(words).view(ml_dtypes.float8_e4m3fn).astype(np.float64)
    else:
        nib = np.empty((g, p, n, 4), np.uint8)
        nib[..., 0::2] = words & 0xF
        nib[..., 1::2] = words >> 4
        vals = E2M1[nib]
    vals = vals * np.repeat(np.exp2(scales.astype(np.float64) - 127.0), 8, axis=1)[..., None]
    return vals.transpose(0, 1, 3, 2).reshape(g * 512, n)
def pack4(w):
    words, scales = pack_weight(w, "e2m1")
    return words.reshape(words.shape[0], 128, -1), scales


def unpack4(words, scales):
    return unpack_weight(words.reshape(words.shape[0], 128, -1, 2), scales, "e2m1")


def planes(Y):
    n, m = Y.shape
    b = f64(bf(Y)).reshape(n // 32, 32, m)
    amax = np.abs(b).max(1)
    byte = np.clip(np.where(amax > 0, np.frexp(amax)[1] - 1 + 127 - 7, 1), 1, 254)
    codes = (b * np.exp2(127.0 - byte)[:, None, :]).reshape(n, m).astype(np.float32).astype(ml_dtypes.float8_e4m3fn).view(np.uint8)
    words = codes.reshape(n // 512, 128, 4, m).transpose(0, 1, 3, 2)
    return np.ascontiguousarray(words), np.ascontiguousarray(byte.astype(np.uint8).reshape(n // 512, 16, m))


M, KS, KV, N = 1024, 1536, 512, 2048

def noise(*shape):
    return np.random.standard_normal(shape)

def setup_inputs():
    s = mx_kscale(KS)
    v = mx_kscale(KV)
    spot = f64(bf(noise(KS, M) * s[:, None]))
    vol = f64(bf(noise(KV, M) * v[:, None]))
    spot_words, spot_scales = pack_weight(spot, "e4m3")
    vol_words, vol_scales = pack_weight(vol, "e4m3")
    deltas = bf(noise(KS, N) / np.sqrt(KS) / s[:, None])
    vegas = bf(noise(KV, N) / np.sqrt(KV) / v[:, None])
    vega_weight = bf(np.exp(0.4 * noise(N)))
    carry = bf(0.5 * noise(N))
    quantity = bf(np.sign(noise(N)) * np.exp(0.8 * noise(N)))
    return {"spot_words": spot_words, "spot_scales": spot_scales,
            "vol_words": vol_words, "vol_scales": vol_scales,
            "deltas": deltas, "vegas": vegas,
            "vega_weight": vega_weight, "carry": carry, "quantity": quantity}

def reference(spot_words, spot_scales, vol_words, vol_scales, deltas, vegas, vega_weight, carry, quantity):
    S = unpack_weight(spot_words, spot_scales, "e4m3")
    V = unpack_weight(vol_words, vol_scales, "e4m3")
    delta_pnl = S.T @ mxq(f64(deltas), 0, "e4m3")
    vega_pnl = V.T @ mxq(f64(vegas), 0, "e4m3")
    y = (delta_pnl + vega_pnl * f64(vega_weight) + f64(carry)) * f64(quantity)
    Y = y.T
    words, scales = planes(Y)
    return y, words, scales

@@ -1,0 +1,306 @@
+from contextlib import ExitStack
+
+import concourse.mybir as mybir
+from concourse.masks import make_identity
+
+M, KS, KV, N = 1024, 1536, 512, 2048
+FLOPS = 2 * M * N * (KS + KV)
+
+F32 = mybir.dt.float32
+BF16 = mybir.dt.bfloat16
+I32 = mybir.dt.int32
+U32 = mybir.dt.uint32
+U8 = mybir.dt.uint8
+FP8X4 = mybir.dt.float8_e4m3fn_x4
+ALU = mybir.AluOpType
+ACT = mybir.ActivationFunctionType
+
+P = 128
+PACK = 4
+GROUP = P * PACK
+GROUPS = N // GROUP
+CHUNKS = (KV + KS) // GROUP
+BANKS = 8
+HALF = 256
+
+
+PARAMS = dict(a=6, e=0, i=19, q=11, x=12, y=4, tpos=2, n0=10, n1=1, n2=1, n3=1, r0=1, r1=1, r2=0, r3=1, Qh=3)
+
+
+def schedule(p=PARAMS):
+    blocks = [(g, m0, 512) for g in range(4) for m0 in (0, 512)][:-1] + [(3, 512, 256), (3, 768, 256)]
+    nb = len(blocks)
+    vs = [("loads", 0, q) for q in range(4)]
+    ss = [("loads", 1, q) for q in range(4)]
+
+    def w(c, g0, g1):
+        return [("loadw", c, g0, g1)]
+
+    def a(mh, c0, c1):
+        return [("loada", mh, c0, c1)]
+
+    rest = w(1, 2, 4) + w(2, 2, 4) + w(3, 2, 4)
+    g1 = w(1, 1, 2) + w(2, 1, 2) + w(3, 1, 2)
+    heads = [
+        w(0, 0, 1) + vs + a(2, 0, 1) + w(1, 0, 1) + w(0, 1, 2) + ss + a(0, 1, 2) + w(2, 0, 1) + a(0, 2, 3) + w(3, 0, 1) + a(0, 3, 4) + a(1, 1, 4) + g1 + w(0, 2, 4) + rest,
+        w(0, 0, 1) + vs + a(2, 0, 1) + w(0, 1, 4) + w(1, 0, 1) + ss + a(0, 1, 2) + w(2, 0, 1) + a(0, 2, 3) + w(3, 0, 1) + a(0, 3, 4) + a(1, 1, 4) + g1 + rest,
+        w(0, 0, 1) + vs + a(2, 0, 1) + w(1, 0, 1) + ss + a(0, 1, 2) + w(2, 0, 1) + a(0, 2, 3) + w(3, 0, 1) + a(0, 3, 4) + w(0, 1, 2) + a(1, 1, 4) + g1 + w(0, 2, 4) + rest,
+        w(0, 0, 2) + vs + a(2, 0, 1) + w(1, 0, 1) + ss + w(2, 0, 1) + a(0, 1, 3) + w(3, 0, 1) + a(0, 3, 4) + a(1, 1, 4) + g1 + w(0, 2, 4) + rest,
+        w(0, 0, 1) + vs + a(0, 0, 1) + w(1, 0, 1) + ss + w(2, 0, 1) + a(0, 1, 3) + w(3, 0, 1) + a(0, 3, 4) + a(1, 0, 1) + w(0, 1, 2) + a(1, 1, 4) + g1 + w(0, 2, 4) + rest,
+        w(0, 0, 1) + vs + a(2, 0, 1) + w(1, 0, 1) + ss + w(2, 0, 1) + a(2, 1, 2) + w(3, 0, 1) + a(2, 2, 3) + a(2, 3, 4) + w(0, 1, 4) + g1 + rest,
+    ]
+    loads = heads[p["Qh"]]
+    on_scalar = [
+        lambda g, c, h: h == 1,
+        lambda g, c, h: h == 1 and c > 0,
+        lambda g, c, h: h == 1 and (c > 0 or g == 0),
+        lambda g, c, h: h == 0,
+        lambda g, c, h: h == 1 and g > 0,
+        lambda g, c, h: h == 1 and (g > 0 or c == 3),
+        lambda g, c, h: h == 1 and not (g == 0 and c in (1, 2)),
+        lambda g, c, h: h == 1 or (c == 1 and g > 0),
+    ][p["a"]]
+    on_vector = [
+        lambda b, i: False,
+        lambda b, i: b == 8 and i == 1,
+        lambda b, i: b >= 6 and i % 2 == 1,
+        lambda b, i: (b >= 6 and i % 2 == 1) or (b % 2 == 1 and i == 3),
+        lambda b, i: i == 3 or (b >= 7 and i == 1),
+        lambda b, i: (b % 2 == 0 and i == 3) or (b >= 7 and i == 1),
+        lambda b, i: (b >= 5 and i == 3) or (b >= 7 and i == 1),
+    ][p["e"]]
+
+    pe = []
+    free = list(range(8))
+    units = [(b, t) for b in range(nb) for t in range(4)]
+
+    def take():
+        return free.pop(0)
+
+    def vega_passes(n):
+        for unit in units[:n]:
+            bank = take()
+            pe.append(("pass", unit[0], unit[1], 0, bank))
+            free.append(bank)
+            units.remove(unit)
+
+    vega_passes(p["n0"])
+    held = [take() for t in range(4)]
+    for c in (1, 2, 3):
+        for t in range(4):
+            pe.append(("pass", 0, t, c, held[t]))
+            if c == 3:
+                free.append(held[t])
+        vega_passes(p["n%d" % c])
+    for b in range(1, nb + 1):
+        for t in range(4):
+            if b < nb:
+                if (b, t) in units:
+                    vega_passes(units.index((b, t)) + 1)
+                bank = take()
+                pe.extend(("pass", b, t, c, bank) for c in (1, 2, 3))
+                free.append(bank)
+                vega_passes(p["r%d" % t])
+            if t == (p["tpos"] if b < nb else 0):
+                for i in range(blocks[b - 1][2] // 128):
+                    bank = take()
+                    pe.append(("turn", b - 1, i, bank))
+                    free.append(bank)
+
+    keyed = []
+    seen = set()
+    for pos, op in enumerate(pe):
+        keyed.append((pos, 0, op))
+        if op[0] == "pass":
+            b, t, c, bank = op[1:]
+            half = (blocks[b][0], c, t // 2)
+            if half not in seen:
+                seen.add(half)
+                keyed.append((pos - max(p["i"], p["q"] + 1), -1, ("inter",) + half + ("S" if on_scalar(*half) else "V",)))
+                keyed.append((pos - p["q"], -1, ("quantw",) + half))
+            if c == 0:
+                keyed.append((pos, 1, ("vega", b, t, bank)))
+            if c == 3:
+                keyed.append((pos, 1, ("delta", b, t, bank)))
+        else:
+            b, i, bank = op[1:]
+            keyed.append((pos, 1, ("evac", b, i, bank, "V" if on_vector(b, i) else "S")))
+            if b == nb - 1:
+                keyed.append((pos, 2, ("storey", b, i, i + 1)))
+            elif i % 2 == 1:
+                keyed.append((pos, 2, ("storey", b, i - 1, i + 1)))
+            if i == 0:
+                lag, gap = (p["x"], p["y"]) if b < nb - 1 else (-1, 1)
+                keyed.append((pos + lag, 3, ("xcopy", b)))
+                keyed.append((pos + lag + gap, 4, ("quanty", b)))
+                keyed.append((pos + lag + gap, 5, ("storew", b)))
+    keyed.sort(key=lambda e: e[:2])
+    ops = loads + [e[2] for e in keyed] + [("stores", q) for q in range(4)]
+    return blocks, ops
+
+
+def tile_delta_vega_scenario_pnl_g6_kernel(
+    tc, spot_words, spot_scales, vol_words, vol_scales, deltas, vegas, vega_weight, carry, quantity,
+    out_0, out_1, out_2,
+):
+    nc = tc.nc
+    blocks, ops = schedule()
+
+    with ExitStack() as ctx:
+        keep = ctx.enter_context(tc.tile_pool(name="keep", bufs=1))
+        work = ctx.enter_context(tc.tile_pool(name="work", bufs=1))
+        psum = ctx.enter_context(tc.psum_pool(name="psum", bufs=1))
+        ctx.enter_context(tc.manual_schedule(engines={mybir.EngineType.PE, mybir.EngineType.SP}))
+
+        banks = [psum.tile([P, GROUP], F32, name="bank%d" % i) for i in range(BANKS)]
+        ident = keep.tile([P, P], F32)
+        a_words = keep.tile([P, CHUNKS, M], U32, align_bytes=256)
+        a_scales = keep.tile([P, CHUNKS, M], U8, align_bytes=256)
+        y_scales = keep.tile([P, M], U8, align_bytes=256)
+        w_codes = {}
+        w_scales = {}
+
+        make_identity(nc, ident[:])
+        vw = keep.tile([P, GROUPS, PACK], BF16)
+        cy = keep.tile([P, GROUPS, PACK], BF16)
+        qt = keep.tile([P, GROUPS, PACK], BF16)
+        for dst, src in ((qt, quantity), (vw, vega_weight), (cy, carry)):
+            nc.gpsimd.dma_start(out=dst[:], in_=src.rearrange("(g p t) -> p g t", g=GROUPS, t=PACK))
+        q32 = keep.tile([P, GROUPS, PACK], F32)
+        vwq = keep.tile([P, GROUPS, PACK], F32)
+        cq = keep.tile([P, GROUPS, PACK], F32)
+        nc.scalar.activation(out=q32[:], in_=qt[:], func=ACT.Identity)
+        nc.gpsimd.tensor_tensor(out=vwq[:], in0=vw[:], in1=qt[:], op=ALU.mult)
+        nc.gpsimd.tensor_tensor(out=cq[:], in0=cy[:], in1=qt[:], op=ALU.mult)
+        nc.vector.memset(a_scales[:].rearrange("p c m -> p (c m)").bitcast(I32), 0)
+
+        spot_w = spot_words.rearrange("g p m t -> p g (m t)").bitcast(I32)
+        vol_w = vol_words.rearrange("g p m t -> p g (m t)").bitcast(I32)
+        out_w = out_1.rearrange("g p m t -> g p (m t)").bitcast(I32)
+
+        raw = {}
+        grouped = {}
+        y_t = {}
+        y_bf = {}
+        y_codes = {}
+        y_out = {}
+
+        for op in ops:
+            kind = op[0]
+            if kind == "loadw":
+                c, g0, g1 = op[1:]
+                src = vegas if c == 0 else deltas[GROUP * (c - 1) : GROUP * c, :]
+                tl = keep.tile([P, PACK, GROUP * (g1 - g0)], BF16, name="raw%d_%d" % (g0, c))
+                nc.sync.dma_start(
+                    out=tl[:], in_=src[:, GROUP * g0 : GROUP * g1].rearrange("(p j) n -> p j n", j=PACK)
+                )
+                for g in range(g0, g1):
+                    raw[g, c] = tl[:, :, GROUP * (g - g0) : GROUP * (g - g0 + 1)]
+            elif kind == "loada":
+                mh, c0, c1 = op[1:]
+                src = vol_w if c0 == 0 else spot_w[:, c0 - 1 : c1 - 1, :]
+                cols = slice(0, M) if mh == 2 else slice(GROUP * mh, GROUP * (mh + 1))
+                nc.sync.dma_start(out=a_words[:, c0:c1, cols].bitcast(I32), in_=src[:, :, cols])
+            elif kind == "loads":
+                spot, q = op[1:]
+                src = spot_scales if spot else vol_scales
+                c0, c1 = (1, CHUNKS) if spot else (0, 1)
+                nc.sync.dma_start(
+                    out=a_scales[32 * q : 32 * q + 4, c0:c1, :].bitcast(I32),
+                    in_=src[:, 4 * q : 4 * q + 4, :].rearrange("g r m -> r g m").bitcast(I32),
+                )
+            elif kind == "inter":
+                g, c, h, eng = op[1:]
+                grouped[g, c, h] = work.tile([P, 2, P, PACK], BF16, name="grouped", bufs=6, align_bytes=256)
+                src = raw[g, c].rearrange("p j (a b t) -> p a j b t", b=2, t=PACK)[:, :, :, :, 2 * h : 2 * h + 2]
+                dst = grouped[g, c, h][:].rearrange("p t (a b) j -> p a j b t", b=2)
+                if eng == "V":
+                    nc.vector.tensor_copy(out=dst, in_=src)
+                else:
+                    nc.scalar.copy(out=dst, in_=src)
+            elif kind == "quantw":
+                g, c, h = op[1:]
+                t0, t1 = 2 * h, 2 * h + 2
+                if (g, c) not in w_codes:
+                    name, bufs = ("vega", 4) if c == 0 else ("delta", 7)
+                    w_codes[g, c] = work.tile([P, GROUP], U32, name=name + "_codes", bufs=bufs, align_bytes=256)
+                    w_scales[g, c] = work.tile([P, GROUP], U8, name=name + "_scales", bufs=bufs, align_bytes=256)
+                nc.vector.quantize_mx(
+                    out=w_codes[g, c][:, P * t0 : P * t1].bitcast(FP8X4),
+                    scales=w_scales[g, c][:, P * t0 : P * t1],
+                    in_=grouped[g, c, h][:].rearrange("p t m j -> p (t m j)"),
+                )
+            elif kind == "pass":
+                b, t, c, bank = op[1:]
+                g, m0, w = blocks[b]
+                nc.tensor.matmul_mx(
+                    out=banks[bank][:, :w],
+                    lhsT=w_codes[g, c][:, P * t : P * (t + 1)].bitcast(FP8X4),
+                    lhsT_scale=w_scales[g, c][:, P * t : P * (t + 1)],
+                    rhs=a_words[:, c, m0 : m0 + w].bitcast(FP8X4),
+                    rhs_scale=a_scales[:, c, m0 : m0 + w],
+                    start=c <= 1,
+                    stop=c in (0, CHUNKS - 1),
+                )
+            elif kind == "vega":
+                b, t, bank = op[1:]
+                g, m0, w = blocks[b]
+                if t == 0:
+                    y_t[b] = work.tile([P, PACK, w], F32, name="y_t" if w == GROUP else "y_t_half", bufs=7 if w == GROUP else 2)
+                nc.scalar.activation(
+                    out=y_t[b][:, t, :], in_=banks[bank][:, :w], func=ACT.Identity,
+                    scale=vwq[:, g, t : t + 1], bias=cq[:, g, t : t + 1],
+                )
+            elif kind == "delta":
+                b, t, bank = op[1:]
+                g, m0, w = blocks[b]
+                nc.vector.scalar_tensor_tensor(
+                    out=y_t[b][:, t, :], in0=banks[bank][:, :w], scalar=q32[:, g, t : t + 1],
+                    in1=y_t[b][:, t, :], op0=ALU.mult, op1=ALU.add,
+                )
+            elif kind == "turn":
+                b, i, bank = op[1:]
+                for t in range(PACK):
+                    nc.tensor.transpose(banks[bank][:, P * t : P * (t + 1)], y_t[b][:, t, P * i : P * (i + 1)], ident[:])
+            elif kind == "evac":
+                b, i, bank, eng = op[1:]
+                if i % 2 == 0:
+                    y_out[b, i // 2] = work.tile([P, 2, GROUP], F32, name="y_out", bufs=5)
+                src = banks[bank][:].rearrange("m (t p) -> m p t", t=PACK)
+                dst = y_out[b, i // 2][:, i % 2, :].rearrange("m (p t) -> m p t", t=PACK)
+                if eng == "V":
+                    nc.vector.tensor_copy(out=dst, in_=src)
+                else:
+                    nc.scalar.copy(out=dst, in_=src)
+            elif kind == "xcopy":
+                b = op[1]
+                g, m0, w = blocks[b]
+                y_bf[b] = work.tile([P, GROUP, PACK], BF16, name="y_bf", bufs=2, align_bytes=256)
+                nc.vector.tensor_copy(
+                    out=y_bf[b][:, :w, :].rearrange("p (a i) t -> p a t i", i=4),
+                    in_=y_t[b][:].rearrange("p t (a i) -> p a t i", i=4),
+                )
+            elif kind == "quanty":
+                b = op[1]
+                g, m0, w = blocks[b]
+                y_codes[b] = work.tile([P, GROUP], U32, name="y_codes", bufs=3, align_bytes=256)
+                nc.vector.quantize_mx(
+                    out=y_codes[b][:, :w].bitcast(FP8X4),
+                    scales=y_scales[4 * g : P, m0 : m0 + w],
+                    in_=y_bf[b][:, :w, :].rearrange("p m t -> p (m t)"),
+                )
+            elif kind == "storew":
+                b = op[1]
+                g, m0, w = blocks[b]
+                nc.sync.dma_start(out=out_w[g, :, m0 : m0 + w], in_=y_codes[b][:, :w].bitcast(I32))
+            elif kind == "storey":
+                b, i0, i1 = op[1:]
+                g, m0, w = blocks[b]
+                rows = out_0[m0 + P * i0 : m0 + P * i1, GROUP * g : GROUP * (g + 1)]
+                nc.sync.dma_start(out=rows.rearrange("(i m) n -> m i n", m=P), in_=y_out[b, i0 // 2][:, i0 % 2 : i0 % 2 + i1 - i0, :])
+            elif kind == "stores":
+                q = op[1]
+                nc.sync.dma_start(
+                    out=out_2[:, 4 * q : 4 * q + 4, :].bitcast(I32),
+                    in_=y_scales[32 * q : 32 * q + 16, :].bitcast(I32),
+                )

@@ -24,13 +24,13 @@ BANKS = 8
 HALF = 256
 
 
-PARAMS = dict(a=6, e=0, i=19, q=11, x=12, y=4, tpos=2, n0=10, n1=1, n2=1, n3=1, r0=1, r1=1, r2=0, r3=1, Qh=3)
+RANGES = dict(xb=(3, 9), xc=(3, 8), a=(12, 32), a0=(12, 32), Qh=(0, 6))
+PARAMS = dict(xb=8, xc=4, a0=22, a=18, e=0, i=23, q=11, x=20, y=2, tpos=2, n0=6, n1=3, n2=1, n3=3, r0=2, r1=0, r2=1, r3=0, Qh=3)
 
 
 def schedule(p=PARAMS):
     blocks = [(g, m0, 512) for g in range(4) for m0 in (0, 512)][:-1] + [(3, 512, 256), (3, 768, 256)]
     nb = len(blocks)
-    vs = [("loads", 0, q) for q in range(4)]
     ss = [("loads", 1, q) for q in range(4)]
 
     def w(c, g0, g1):
@@ -41,25 +41,17 @@ def schedule(p=PARAMS):
 
     rest = w(1, 2, 4) + w(2, 2, 4) + w(3, 2, 4)
     g1 = w(1, 1, 2) + w(2, 1, 2) + w(3, 1, 2)
+    vs = [("loads", 0, q) for q in range(4)]
     heads = [
-        w(0, 0, 1) + vs + a(2, 0, 1) + w(1, 0, 1) + w(0, 1, 2) + ss + a(0, 1, 2) + w(2, 0, 1) + a(0, 2, 3) + w(3, 0, 1) + a(0, 3, 4) + a(1, 1, 4) + g1 + w(0, 2, 4) + rest,
-        w(0, 0, 1) + vs + a(2, 0, 1) + w(0, 1, 4) + w(1, 0, 1) + ss + a(0, 1, 2) + w(2, 0, 1) + a(0, 2, 3) + w(3, 0, 1) + a(0, 3, 4) + a(1, 1, 4) + g1 + rest,
-        w(0, 0, 1) + vs + a(2, 0, 1) + w(1, 0, 1) + ss + a(0, 1, 2) + w(2, 0, 1) + a(0, 2, 3) + w(3, 0, 1) + a(0, 3, 4) + w(0, 1, 2) + a(1, 1, 4) + g1 + w(0, 2, 4) + rest,
-        w(0, 0, 2) + vs + a(2, 0, 1) + w(1, 0, 1) + ss + w(2, 0, 1) + a(0, 1, 3) + w(3, 0, 1) + a(0, 3, 4) + a(1, 1, 4) + g1 + w(0, 2, 4) + rest,
-        w(0, 0, 1) + vs + a(0, 0, 1) + w(1, 0, 1) + ss + w(2, 0, 1) + a(0, 1, 3) + w(3, 0, 1) + a(0, 3, 4) + a(1, 0, 1) + w(0, 1, 2) + a(1, 1, 4) + g1 + w(0, 2, 4) + rest,
-        w(0, 0, 1) + vs + a(2, 0, 1) + w(1, 0, 1) + ss + w(2, 0, 1) + a(2, 1, 2) + w(3, 0, 1) + a(2, 2, 3) + a(2, 3, 4) + w(0, 1, 4) + g1 + rest,
+        w(0, 0, 1) + a(2, 0, 1) + w(1, 0, 1) + vs + w(0, 1, 2) + a(0, 1, 2) + ss + w(2, 0, 1) + a(0, 2, 3) + w(3, 0, 1) + a(0, 3, 4) + a(1, 1, 4) + g1 + w(0, 2, 4) + rest,
+        w(0, 0, 1) + w(0, 1, 2) + a(2, 0, 1) + vs + w(1, 0, 1) + w(2, 0, 1) + ss + a(0, 1, 3) + w(3, 0, 1) + a(0, 3, 4) + a(1, 1, 4) + g1 + w(0, 2, 4) + rest,
+        w(0, 0, 1) + a(2, 0, 1) + w(1, 0, 1) + vs + a(0, 1, 2) + w(2, 0, 1) + ss + a(0, 2, 3) + w(3, 0, 1) + a(0, 3, 4) + w(0, 1, 2) + a(1, 1, 4) + g1 + w(0, 2, 4) + rest,
+        w(0, 0, 2) + a(2, 0, 1) + w(1, 0, 1) + vs + w(2, 0, 1) + a(0, 1, 3) + ss + w(3, 0, 1) + a(0, 3, 4) + a(1, 1, 4) + g1 + w(0, 2, 4) + rest,
+        w(0, 0, 2) + a(2, 0, 1) + w(1, 0, 1) + vs + w(2, 0, 1) + w(3, 0, 1) + ss + a(0, 1, 4) + a(1, 1, 4) + g1 + w(0, 2, 4) + rest,
+        w(0, 0, 2) + a(2, 0, 1) + w(1, 0, 2) + vs + a(2, 1, 2) + ss + w(2, 0, 2) + a(2, 2, 3) + w(3, 0, 2) + a(2, 3, 4) + w(0, 2, 4) + rest,
+        w(0, 0, 1) + a(2, 0, 1) + w(0, 1, 2) + vs + w(1, 0, 1) + w(2, 0, 1) + ss + a(0, 1, 3) + w(3, 0, 1) + a(0, 3, 4) + a(1, 1, 4) + g1 + w(0, 2, 4) + rest,
     ]
     loads = heads[p["Qh"]]
-    on_scalar = [
-        lambda g, c, h: h == 1,
-        lambda g, c, h: h == 1 and c > 0,
-        lambda g, c, h: h == 1 and (c > 0 or g == 0),
-        lambda g, c, h: h == 0,
-        lambda g, c, h: h == 1 and g > 0,
-        lambda g, c, h: h == 1 and (g > 0 or c == 3),
-        lambda g, c, h: h == 1 and not (g == 0 and c in (1, 2)),
-        lambda g, c, h: h == 1 or (c == 1 and g > 0),
-    ][p["a"]]
     on_vector = [
         lambda b, i: False,
         lambda b, i: b == 8 and i == 1,
@@ -113,11 +105,15 @@ def schedule(p=PARAMS):
         keyed.append((pos, 0, op))
         if op[0] == "pass":
             b, t, c, bank = op[1:]
-            half = (blocks[b][0], c, t // 2)
-            if half not in seen:
-                seen.add(half)
-                keyed.append((pos - max(p["i"], p["q"] + 1), -1, ("inter",) + half + ("S" if on_scalar(*half) else "V",)))
-                keyed.append((pos - p["q"], -1, ("quantw",) + half))
+            chunk = (blocks[b][0], c)
+            if chunk not in seen:
+                seen.add(chunk)
+                cut = 2 * (p["a0"] if chunk[0] == 0 else p["a"])
+                lead = max(p["i"], p["q"] + 1)
+                keyed.append((pos - lead, -1, ("inter",) + chunk + (0, cut, "V")))
+                if cut < 64:
+                    keyed.append((pos - lead, -1, ("inter",) + chunk + (cut, 64, "S")))
+                keyed.append((pos - p["q"], -1, ("quantw",) + chunk))
             if c == 0:
                 keyed.append((pos, 1, ("vega", b, t, bank)))
             if c == 3:
@@ -131,7 +127,10 @@ def schedule(p=PARAMS):
                 keyed.append((pos, 2, ("storey", b, i - 1, i + 1)))
             if i == 0:
                 lag, gap = (p["x"], p["y"]) if b < nb - 1 else (-1, 1)
-                keyed.append((pos + lag, 3, ("xcopy", b)))
+                cut = p["xc"] if b >= p["xb"] else 8
+                keyed.append((pos + lag, 3, ("xcopy", b, 0, cut, "V")))
+                if cut < 8:
+                    keyed.append((pos + lag, 3, ("xcopy", b, cut, 8, "S")))
                 keyed.append((pos + lag + gap, 4, ("quanty", b)))
                 keyed.append((pos + lag + gap, 5, ("storew", b)))
     keyed.sort(key=lambda e: e[:2])
@@ -150,7 +149,7 @@ def tile_delta_vega_scenario_pnl_g6_kernel(
         keep = ctx.enter_context(tc.tile_pool(name="keep", bufs=1))
         work = ctx.enter_context(tc.tile_pool(name="work", bufs=1))
         psum = ctx.enter_context(tc.psum_pool(name="psum", bufs=1))
-        ctx.enter_context(tc.manual_schedule(engines={mybir.EngineType.PE, mybir.EngineType.SP}))
+        ctx.enter_context(tc.manual_schedule(engines={mybir.EngineType.PE, mybir.EngineType.SP, mybir.EngineType.Pool}))
 
         banks = [psum.tile([P, GROUP], F32, name="bank%d" % i) for i in range(BANKS)]
         ident = keep.tile([P, P], F32)
@@ -160,19 +159,27 @@ def tile_delta_vega_scenario_pnl_g6_kernel(
         w_codes = {}
         w_scales = {}
 
+        rows = keep.tile([P, GROUP], BF16)
+        nc.vector.memset(rows[:].bitcast(I32), 0)
+        nc.vector.memset(a_scales[:].rearrange("p c m -> p (c m)").bitcast(I32), 0)
         make_identity(nc, ident[:])
-        vw = keep.tile([P, GROUPS, PACK], BF16)
-        cy = keep.tile([P, GROUPS, PACK], BF16)
-        qt = keep.tile([P, GROUPS, PACK], BF16)
-        for dst, src in ((qt, quantity), (vw, vega_weight), (cy, carry)):
-            nc.gpsimd.dma_start(out=dst[:], in_=src.rearrange("(g p t) -> p g t", g=GROUPS, t=PACK))
+        for k, src in enumerate((quantity, vega_weight, carry)):
+            nc.scalar.dma_start(out=rows[GROUPS * k : GROUPS * (k + 1), :], in_=src.rearrange("(g n) -> g n", g=GROUPS))
+        pairs = rows[:].bitcast(F32)
+        for u in range(2):
+            nc.tensor.transpose(banks[BANKS - 1][:, P * u : P * (u + 1)], pairs[:, u : 2 * P : 2], ident[:])
+        vec = keep.tile([P, 3 * GROUPS, PACK], BF16)
+        nc.vector.tensor_copy(
+            out=vec[:].bitcast(F32),
+            in_=banks[BANKS - 1][:, : 2 * P].rearrange("p (u x) -> p x u", u=2)[:, : 3 * GROUPS, :],
+        )
+        qt, vw, cy = (vec[:, GROUPS * k : GROUPS * (k + 1), :] for k in range(3))
         q32 = keep.tile([P, GROUPS, PACK], F32)
         vwq = keep.tile([P, GROUPS, PACK], F32)
         cq = keep.tile([P, GROUPS, PACK], F32)
-        nc.scalar.activation(out=q32[:], in_=qt[:], func=ACT.Identity)
-        nc.gpsimd.tensor_tensor(out=vwq[:], in0=vw[:], in1=qt[:], op=ALU.mult)
-        nc.gpsimd.tensor_tensor(out=cq[:], in0=cy[:], in1=qt[:], op=ALU.mult)
-        nc.vector.memset(a_scales[:].rearrange("p c m -> p (c m)").bitcast(I32), 0)
+        nc.scalar.activation(out=q32[:], in_=qt, func=ACT.Identity)
+        nc.vector.tensor_tensor(out=vwq[:], in0=vw, in1=qt, op=ALU.mult)
+        nc.vector.tensor_tensor(out=cq[:], in0=cy, in1=qt, op=ALU.mult)
 
         spot_w = spot_words.rearrange("g p m t -> p g (m t)").bitcast(I32)
         vol_w = vol_words.rearrange("g p m t -> p g (m t)").bitcast(I32)
@@ -210,25 +217,24 @@ def tile_delta_vega_scenario_pnl_g6_kernel(
                     in_=src[:, 4 * q : 4 * q + 4, :].rearrange("g r m -> r g m").bitcast(I32),
                 )
             elif kind == "inter":
-                g, c, h, eng = op[1:]
-                grouped[g, c, h] = work.tile([P, 2, P, PACK], BF16, name="grouped", bufs=6, align_bytes=256)
-                src = raw[g, c].rearrange("p j (a b t) -> p a j b t", b=2, t=PACK)[:, :, :, :, 2 * h : 2 * h + 2]
-                dst = grouped[g, c, h][:].rearrange("p t (a b) j -> p a j b t", b=2)
+                g, c, a0, a1, eng = op[1:]
+                if (g, c) not in grouped:
+                    grouped[g, c] = work.tile([P, PACK, P, PACK], BF16, name="grouped", bufs=3, align_bytes=256)
+                src = raw[g, c].rearrange("p j (a b t) -> p a j b t", b=2, t=PACK)[:, a0:a1]
+                dst = grouped[g, c][:].rearrange("p t (a b) j -> p a j b t", b=2)[:, a0:a1]
                 if eng == "V":
                     nc.vector.tensor_copy(out=dst, in_=src)
                 else:
                     nc.scalar.copy(out=dst, in_=src)
             elif kind == "quantw":
-                g, c, h = op[1:]
-                t0, t1 = 2 * h, 2 * h + 2
-                if (g, c) not in w_codes:
-                    name, bufs = ("vega", 4) if c == 0 else ("delta", 7)
-                    w_codes[g, c] = work.tile([P, GROUP], U32, name=name + "_codes", bufs=bufs, align_bytes=256)
-                    w_scales[g, c] = work.tile([P, GROUP], U8, name=name + "_scales", bufs=bufs, align_bytes=256)
+                g, c = op[1:]
+                name, bufs = ("vega", 4) if c == 0 else ("delta", 7)
+                w_codes[g, c] = work.tile([P, GROUP], U32, name=name + "_codes", bufs=bufs, align_bytes=256)
+                w_scales[g, c] = work.tile([P, GROUP], U8, name=name + "_scales", bufs=bufs, align_bytes=256)
                 nc.vector.quantize_mx(
-                    out=w_codes[g, c][:, P * t0 : P * t1].bitcast(FP8X4),
-                    scales=w_scales[g, c][:, P * t0 : P * t1],
-                    in_=grouped[g, c, h][:].rearrange("p t m j -> p (t m j)"),
+                    out=w_codes[g, c][:].bitcast(FP8X4),
+                    scales=w_scales[g, c][:],
+                    in_=grouped[g, c][:].rearrange("p t m j -> p (t m j)"),
                 )
             elif kind == "pass":
                 b, t, c, bank = op[1:]
@@ -273,13 +279,17 @@ def tile_delta_vega_scenario_pnl_g6_kernel(
                 else:
                     nc.scalar.copy(out=dst, in_=src)
             elif kind == "xcopy":
-                b = op[1]
+                b, e0, e1, eng = op[1:]
                 g, m0, w = blocks[b]
-                y_bf[b] = work.tile([P, GROUP, PACK], BF16, name="y_bf", bufs=2, align_bytes=256)
-                nc.vector.tensor_copy(
-                    out=y_bf[b][:, :w, :].rearrange("p (a i) t -> p a t i", i=4),
-                    in_=y_t[b][:].rearrange("p t (a i) -> p a t i", i=4),
-                )
+                if e0 == 0:
+                    y_bf[b] = work.tile([P, GROUP, PACK], BF16, name="y_bf", bufs=2, align_bytes=256)
+                cols = slice(w * e0 // 8, w * e1 // 8)
+                src = y_t[b][:, :, cols].rearrange("p t (a i) -> p a t i", i=4)
+                dst = y_bf[b][:, cols, :].rearrange("p (a i) t -> p a t i", i=4)
+                if eng == "V":
+                    nc.vector.tensor_copy(out=dst, in_=src)
+                else:
+                    nc.scalar.copy(out=dst, in_=src)
             elif kind == "quanty":
                 b = op[1]
                 g, m0, w = blocks[b]

@@ -14,128 +14,33 @@ U8 = mybir.dt.uint8
 FP8X4 = mybir.dt.float8_e4m3fn_x4
 ALU = mybir.AluOpType
 ACT = mybir.ActivationFunctionType
+ENGINE = mybir.EngineType
 
 P = 128
 PACK = 4
 GROUP = P * PACK
 GROUPS = N // GROUP
 CHUNKS = (KV + KS) // GROUP
+DELTA_CHUNKS = (1, 2, 3)
+QUADRANTS = 4
 BANKS = 8
-HALF = 256
 
+BLOCKS = [(g, m0, GROUP) for g in range(GROUPS) for m0 in (0, GROUP)][:-1] + [
+    (GROUPS - 1, GROUP, GROUP // 2),
+    (GROUPS - 1, GROUP + GROUP // 2, GROUP // 2),
+]
+LAST = len(BLOCKS) - 1
 
-RANGES = dict(xb=(3, 9), xc=(3, 8), a=(12, 32), a0=(12, 32), Qh=(0, 6))
-PARAMS = dict(xb=8, xc=4, a0=22, a=18, e=0, i=23, q=11, x=20, y=2, tpos=2, n0=6, n1=3, n2=1, n3=3, r0=2, r1=0, r2=1, r3=0, Qh=3)
-
-
-def schedule(p=PARAMS):
-    blocks = [(g, m0, 512) for g in range(4) for m0 in (0, 512)][:-1] + [(3, 512, 256), (3, 768, 256)]
-    nb = len(blocks)
-    ss = [("loads", 1, q) for q in range(4)]
-
-    def w(c, g0, g1):
-        return [("loadw", c, g0, g1)]
-
-    def a(mh, c0, c1):
-        return [("loada", mh, c0, c1)]
-
-    rest = w(1, 2, 4) + w(2, 2, 4) + w(3, 2, 4)
-    g1 = w(1, 1, 2) + w(2, 1, 2) + w(3, 1, 2)
-    vs = [("loads", 0, q) for q in range(4)]
-    heads = [
-        w(0, 0, 1) + a(2, 0, 1) + w(1, 0, 1) + vs + w(0, 1, 2) + a(0, 1, 2) + ss + w(2, 0, 1) + a(0, 2, 3) + w(3, 0, 1) + a(0, 3, 4) + a(1, 1, 4) + g1 + w(0, 2, 4) + rest,
-        w(0, 0, 1) + w(0, 1, 2) + a(2, 0, 1) + vs + w(1, 0, 1) + w(2, 0, 1) + ss + a(0, 1, 3) + w(3, 0, 1) + a(0, 3, 4) + a(1, 1, 4) + g1 + w(0, 2, 4) + rest,
-        w(0, 0, 1) + a(2, 0, 1) + w(1, 0, 1) + vs + a(0, 1, 2) + w(2, 0, 1) + ss + a(0, 2, 3) + w(3, 0, 1) + a(0, 3, 4) + w(0, 1, 2) + a(1, 1, 4) + g1 + w(0, 2, 4) + rest,
-        w(0, 0, 2) + a(2, 0, 1) + w(1, 0, 1) + vs + w(2, 0, 1) + a(0, 1, 3) + ss + w(3, 0, 1) + a(0, 3, 4) + a(1, 1, 4) + g1 + w(0, 2, 4) + rest,
-        w(0, 0, 2) + a(2, 0, 1) + w(1, 0, 1) + vs + w(2, 0, 1) + w(3, 0, 1) + ss + a(0, 1, 4) + a(1, 1, 4) + g1 + w(0, 2, 4) + rest,
-        w(0, 0, 2) + a(2, 0, 1) + w(1, 0, 2) + vs + a(2, 1, 2) + ss + w(2, 0, 2) + a(2, 2, 3) + w(3, 0, 2) + a(2, 3, 4) + w(0, 2, 4) + rest,
-        w(0, 0, 1) + a(2, 0, 1) + w(0, 1, 2) + vs + w(1, 0, 1) + w(2, 0, 1) + ss + a(0, 1, 3) + w(3, 0, 1) + a(0, 3, 4) + a(1, 1, 4) + g1 + w(0, 2, 4) + rest,
-    ]
-    loads = heads[p["Qh"]]
-    on_vector = [
-        lambda b, i: False,
-        lambda b, i: b == 8 and i == 1,
-        lambda b, i: b >= 6 and i % 2 == 1,
-        lambda b, i: (b >= 6 and i % 2 == 1) or (b % 2 == 1 and i == 3),
-        lambda b, i: i == 3 or (b >= 7 and i == 1),
-        lambda b, i: (b % 2 == 0 and i == 3) or (b >= 7 and i == 1),
-        lambda b, i: (b >= 5 and i == 3) or (b >= 7 and i == 1),
-    ][p["e"]]
-
-    pe = []
-    free = list(range(8))
-    units = [(b, t) for b in range(nb) for t in range(4)]
-
-    def take():
-        return free.pop(0)
-
-    def vega_passes(n):
-        for unit in units[:n]:
-            bank = take()
-            pe.append(("pass", unit[0], unit[1], 0, bank))
-            free.append(bank)
-            units.remove(unit)
-
-    vega_passes(p["n0"])
-    held = [take() for t in range(4)]
-    for c in (1, 2, 3):
-        for t in range(4):
-            pe.append(("pass", 0, t, c, held[t]))
-            if c == 3:
-                free.append(held[t])
-        vega_passes(p["n%d" % c])
-    for b in range(1, nb + 1):
-        for t in range(4):
-            if b < nb:
-                if (b, t) in units:
-                    vega_passes(units.index((b, t)) + 1)
-                bank = take()
-                pe.extend(("pass", b, t, c, bank) for c in (1, 2, 3))
-                free.append(bank)
-                vega_passes(p["r%d" % t])
-            if t == (p["tpos"] if b < nb else 0):
-                for i in range(blocks[b - 1][2] // 128):
-                    bank = take()
-                    pe.append(("turn", b - 1, i, bank))
-                    free.append(bank)
-
-    keyed = []
-    seen = set()
-    for pos, op in enumerate(pe):
-        keyed.append((pos, 0, op))
-        if op[0] == "pass":
-            b, t, c, bank = op[1:]
-            chunk = (blocks[b][0], c)
-            if chunk not in seen:
-                seen.add(chunk)
-                cut = 2 * (p["a0"] if chunk[0] == 0 else p["a"])
-                lead = max(p["i"], p["q"] + 1)
-                keyed.append((pos - lead, -1, ("inter",) + chunk + (0, cut, "V")))
-                if cut < 64:
-                    keyed.append((pos - lead, -1, ("inter",) + chunk + (cut, 64, "S")))
-                keyed.append((pos - p["q"], -1, ("quantw",) + chunk))
-            if c == 0:
-                keyed.append((pos, 1, ("vega", b, t, bank)))
-            if c == 3:
-                keyed.append((pos, 1, ("delta", b, t, bank)))
-        else:
-            b, i, bank = op[1:]
-            keyed.append((pos, 1, ("evac", b, i, bank, "V" if on_vector(b, i) else "S")))
-            if b == nb - 1:
-                keyed.append((pos, 2, ("storey", b, i, i + 1)))
-            elif i % 2 == 1:
-                keyed.append((pos, 2, ("storey", b, i - 1, i + 1)))
-            if i == 0:
-                lag, gap = (p["x"], p["y"]) if b < nb - 1 else (-1, 1)
-                cut = p["xc"] if b >= p["xb"] else 8
-                keyed.append((pos + lag, 3, ("xcopy", b, 0, cut, "V")))
-                if cut < 8:
-                    keyed.append((pos + lag, 3, ("xcopy", b, cut, 8, "S")))
-                keyed.append((pos + lag + gap, 4, ("quanty", b)))
-                keyed.append((pos + lag + gap, 5, ("storew", b)))
-    keyed.sort(key=lambda e: e[:2])
-    ops = loads + [e[2] for e in keyed] + [("stores", q) for q in range(4)]
-    return blocks, ops
+RUNS = GROUP // 8
+VECTOR_RUNS = 32
+HEAD_CHUNKS = (((0, 0), 40), ((1, 0), 40), ((0, 1), RUNS), ((0, 2), RUNS), ((0, 3), 48))
+LATER_CHUNKS = [(1, c) for c in DELTA_CHUNKS] + [(g, c) for g in (2, 3) for c in range(CHUNKS)]
+CHUNKS_AFTER_BLOCK = (2, 2, 2, 2, 1, 2)
+VEGA_AFTER_BLOCK = (2, 2, 4, 4, 0, 4, 4, 4)
+CHUNK_OUTER_BLOCKS = (2, 6)
+GPSIMD_SCENARIOS = (256, 256, 256, 256, 256, 384, 128, 256)
+VECTOR_EMPTIES_LAST_BANK = (5, 7)
+FINE_STORES_FROM = 6
 
 
 def tile_delta_vega_scenario_pnl_g6_kernel(
@@ -143,28 +48,27 @@ def tile_delta_vega_scenario_pnl_g6_kernel(
     out_0, out_1, out_2,
 ):
     nc = tc.nc
-    blocks, ops = schedule()
 
     with ExitStack() as ctx:
         keep = ctx.enter_context(tc.tile_pool(name="keep", bufs=1))
         work = ctx.enter_context(tc.tile_pool(name="work", bufs=1))
         psum = ctx.enter_context(tc.psum_pool(name="psum", bufs=1))
-        ctx.enter_context(tc.manual_schedule(engines={mybir.EngineType.PE, mybir.EngineType.SP, mybir.EngineType.Pool}))
+        ctx.enter_context(tc.manual_schedule(engines={ENGINE.PE, ENGINE.SP, ENGINE.Pool, ENGINE.DVE}))
 
         banks = [psum.tile([P, GROUP], F32, name="bank%d" % i) for i in range(BANKS)]
         ident = keep.tile([P, P], F32)
         a_words = keep.tile([P, CHUNKS, M], U32, align_bytes=256)
         a_scales = keep.tile([P, CHUNKS, M], U8, align_bytes=256)
         y_scales = keep.tile([P, M], U8, align_bytes=256)
-        w_codes = {}
-        w_scales = {}
 
         rows = keep.tile([P, GROUP], BF16)
         nc.vector.memset(rows[:].bitcast(I32), 0)
         nc.vector.memset(a_scales[:].rearrange("p c m -> p (c m)").bitcast(I32), 0)
         make_identity(nc, ident[:])
-        for k, src in enumerate((quantity, vega_weight, carry)):
-            nc.scalar.dma_start(out=rows[GROUPS * k : GROUPS * (k + 1), :], in_=src.rearrange("(g n) -> g n", g=GROUPS))
+        for k, vector in enumerate((quantity, vega_weight, carry)):
+            nc.scalar.dma_start(
+                out=rows[GROUPS * k : GROUPS * (k + 1), :], in_=vector.rearrange("(g n) -> g n", g=GROUPS)
+            )
         pairs = rows[:].bitcast(F32)
         for u in range(2):
             nc.tensor.transpose(banks[BANKS - 1][:, P * u : P * (u + 1)], pairs[:, u : 2 * P : 2], ident[:])
@@ -187,130 +91,240 @@ def tile_delta_vega_scenario_pnl_g6_kernel(
 
         raw = {}
         grouped = {}
+        w_codes = {}
+        w_scales = {}
         y_t = {}
-        y_bf = {}
         y_codes = {}
         y_out = {}
+        y_bf = keep.tile([P, GROUP, PACK], BF16, align_bytes=256)
 
-        for op in ops:
-            kind = op[0]
-            if kind == "loadw":
-                c, g0, g1 = op[1:]
-                src = vegas if c == 0 else deltas[GROUP * (c - 1) : GROUP * c, :]
-                tl = keep.tile([P, PACK, GROUP * (g1 - g0)], BF16, name="raw%d_%d" % (g0, c))
-                nc.sync.dma_start(
-                    out=tl[:], in_=src[:, GROUP * g0 : GROUP * g1].rearrange("(p j) n -> p j n", j=PACK)
-                )
-                for g in range(g0, g1):
-                    raw[g, c] = tl[:, :, GROUP * (g - g0) : GROUP * (g - g0 + 1)]
-            elif kind == "loada":
-                mh, c0, c1 = op[1:]
-                src = vol_w if c0 == 0 else spot_w[:, c0 - 1 : c1 - 1, :]
-                cols = slice(0, M) if mh == 2 else slice(GROUP * mh, GROUP * (mh + 1))
-                nc.sync.dma_start(out=a_words[:, c0:c1, cols].bitcast(I32), in_=src[:, :, cols])
-            elif kind == "loads":
-                spot, q = op[1:]
-                src = spot_scales if spot else vol_scales
-                c0, c1 = (1, CHUNKS) if spot else (0, 1)
+        def load_weights(c, g0, g1):
+            src = vegas if c == 0 else deltas[GROUP * (c - 1) : GROUP * c, :]
+            tile = keep.tile([P, PACK, GROUP * (g1 - g0)], BF16, name="raw%d_%d" % (g0, c))
+            nc.sync.dma_start(
+                out=tile[:], in_=src[:, GROUP * g0 : GROUP * g1].rearrange("(p j) n -> p j n", j=PACK)
+            )
+            for g in range(g0, g1):
+                raw[g, c] = tile[:, :, GROUP * (g - g0) : GROUP * (g - g0 + 1)]
+
+        def load_words(c0, c1, m0, m1):
+            src = vol_w if c0 == 0 else spot_w[:, c0 - 1 : c1 - 1, :]
+            nc.sync.dma_start(out=a_words[:, c0:c1, m0:m1].bitcast(I32), in_=src[:, :, m0:m1])
+
+        def load_scales(src, c0, c1):
+            for q in range(QUADRANTS):
                 nc.sync.dma_start(
                     out=a_scales[32 * q : 32 * q + 4, c0:c1, :].bitcast(I32),
                     in_=src[:, 4 * q : 4 * q + 4, :].rearrange("g r m -> r g m").bitcast(I32),
                 )
-            elif kind == "inter":
-                g, c, a0, a1, eng = op[1:]
-                if (g, c) not in grouped:
-                    grouped[g, c] = work.tile([P, PACK, P, PACK], BF16, name="grouped", bufs=3, align_bytes=256)
-                src = raw[g, c].rearrange("p j (a b t) -> p a j b t", b=2, t=PACK)[:, a0:a1]
-                dst = grouped[g, c][:].rearrange("p t (a b) j -> p a j b t", b=2)[:, a0:a1]
-                if eng == "V":
-                    nc.vector.tensor_copy(out=dst, in_=src)
-                else:
-                    nc.scalar.copy(out=dst, in_=src)
-            elif kind == "quantw":
-                g, c = op[1:]
-                name, bufs = ("vega", 4) if c == 0 else ("delta", 7)
-                w_codes[g, c] = work.tile([P, GROUP], U32, name=name + "_codes", bufs=bufs, align_bytes=256)
-                w_scales[g, c] = work.tile([P, GROUP], U8, name=name + "_scales", bufs=bufs, align_bytes=256)
-                nc.vector.quantize_mx(
-                    out=w_codes[g, c][:].bitcast(FP8X4),
-                    scales=w_scales[g, c][:],
-                    in_=grouped[g, c][:].rearrange("p t m j -> p (t m j)"),
-                )
-            elif kind == "pass":
-                b, t, c, bank = op[1:]
-                g, m0, w = blocks[b]
-                nc.tensor.matmul_mx(
-                    out=banks[bank][:, :w],
-                    lhsT=w_codes[g, c][:, P * t : P * (t + 1)].bitcast(FP8X4),
-                    lhsT_scale=w_scales[g, c][:, P * t : P * (t + 1)],
-                    rhs=a_words[:, c, m0 : m0 + w].bitcast(FP8X4),
-                    rhs_scale=a_scales[:, c, m0 : m0 + w],
-                    start=c <= 1,
-                    stop=c in (0, CHUNKS - 1),
-                )
-            elif kind == "vega":
-                b, t, bank = op[1:]
-                g, m0, w = blocks[b]
+
+        def copy_on(engine, dst, src):
+            if engine == "vector":
+                nc.vector.tensor_copy(out=dst, in_=src)
+            else:
+                nc.scalar.copy(out=dst, in_=src)
+
+        def interleave(key, engine, vector_runs):
+            lo, hi = (0, vector_runs) if engine == "vector" else (vector_runs, RUNS)
+            if lo == hi:
+                return
+            if key == LATER_CHUNKS[CHUNKS_AFTER_BLOCK[0] - 1]:
+                grouped[key] = y_bf[:].rearrange("p (t m) j -> p t m j", t=PACK)
+            elif key not in grouped:
+                grouped[key] = work.tile([P, PACK, P, PACK], BF16, name="grouped", bufs=4, align_bytes=256)
+            src = raw[key].rearrange("p j (a b t) -> p a j b t", b=2, t=PACK)[:, lo:hi]
+            dst = grouped[key][:].rearrange("p t (a b) j -> p a j b t", b=2)[:, lo:hi]
+            copy_on(engine, dst, src)
+
+        def quantize_weights(key):
+            name, bufs = ("vega", GROUPS) if key[1] == 0 else ("delta", 7)
+            w_codes[key] = work.tile([P, GROUP], U32, name=name + "_codes", bufs=bufs, align_bytes=256)
+            w_scales[key] = work.tile([P, GROUP], U8, name=name + "_scales", bufs=bufs, align_bytes=256)
+            nc.vector.quantize_mx(
+                out=w_codes[key][:].bitcast(FP8X4),
+                scales=w_scales[key][:],
+                in_=grouped[key][:].rearrange("p t m j -> p (t m j)"),
+            )
+
+        def mx_pass(b, t, c, bank):
+            g, m0, w = BLOCKS[b]
+            nc.tensor.matmul_mx(
+                out=banks[bank][:, :w],
+                lhsT=w_codes[g, c][:, P * t : P * (t + 1)].bitcast(FP8X4),
+                lhsT_scale=w_scales[g, c][:, P * t : P * (t + 1)],
+                rhs=a_words[:, c, m0 : m0 + w].bitcast(FP8X4),
+                rhs_scale=a_scales[:, c, m0 : m0 + w],
+                start=c in (0, DELTA_CHUNKS[0]),
+                stop=c in (0, DELTA_CHUNKS[-1]),
+            )
+
+        free = list(range(BANKS))
+        vega_todo = [(b, t) for b in range(len(BLOCKS)) for t in range(PACK)]
+
+        def vega_passes(count):
+            for b, t in vega_todo[:count]:
+                g, m0, w = BLOCKS[b]
+                bank = free.pop(0)
+                mx_pass(b, t, 0, bank)
                 if t == 0:
-                    y_t[b] = work.tile([P, PACK, w], F32, name="y_t" if w == GROUP else "y_t_half", bufs=7 if w == GROUP else 2)
+                    name, bufs = ("y_t", 7) if w == GROUP else ("y_t_half", 2)
+                    y_t[b] = work.tile([P, PACK, w], F32, name=name, bufs=bufs)
                 nc.scalar.activation(
                     out=y_t[b][:, t, :], in_=banks[bank][:, :w], func=ACT.Identity,
                     scale=vwq[:, g, t : t + 1], bias=cq[:, g, t : t + 1],
                 )
-            elif kind == "delta":
-                b, t, bank = op[1:]
-                g, m0, w = blocks[b]
-                nc.vector.scalar_tensor_tensor(
-                    out=y_t[b][:, t, :], in0=banks[bank][:, :w], scalar=q32[:, g, t : t + 1],
-                    in1=y_t[b][:, t, :], op0=ALU.mult, op1=ALU.add,
-                )
-            elif kind == "turn":
-                b, i, bank = op[1:]
+                free.append(bank)
+                vega_todo.remove((b, t))
+
+        def add_delta(b, t, bank):
+            g, m0, w = BLOCKS[b]
+            nc.vector.scalar_tensor_tensor(
+                out=y_t[b][:, t, :], in0=banks[bank][:, :w], scalar=q32[:, g, t : t + 1],
+                in1=y_t[b][:, t, :], op0=ALU.mult, op1=ALU.add,
+            )
+
+        def empty_bank(b, i, bank, engine):
+            if i % 2 == 0:
+                y_out[b, i // 2] = work.tile([P, 2, GROUP], F32, name="y_out", bufs=5)
+            src = banks[bank][:].rearrange("m (t p) -> m p t", t=PACK)
+            dst = y_out[b, i // 2][:, i % 2, :].rearrange("m (p t) -> m p t", t=PACK)
+            copy_on(engine, dst, src)
+
+        def store_y(b, i0, i1):
+            g, m0, w = BLOCKS[b]
+            dst = out_0[m0 + P * i0 : m0 + P * i1, GROUP * g : GROUP * (g + 1)]
+            nc.sync.dma_start(
+                out=dst.rearrange("(i m) n -> m i n", m=P),
+                in_=y_out[b, i0 // 2][:, i0 % 2 : i0 % 2 + i1 - i0, :],
+            )
+
+        def turn_and_store(b):
+            tiles = BLOCKS[b][2] // P
+            on_scalar = tiles - 1 if b in VECTOR_EMPTIES_LAST_BANK else tiles
+            step = 1 if b >= FINE_STORES_FROM else 2
+            for i in range(tiles):
+                bank = free.pop(0)
                 for t in range(PACK):
-                    nc.tensor.transpose(banks[bank][:, P * t : P * (t + 1)], y_t[b][:, t, P * i : P * (i + 1)], ident[:])
-            elif kind == "evac":
-                b, i, bank, eng = op[1:]
-                if i % 2 == 0:
-                    y_out[b, i // 2] = work.tile([P, 2, GROUP], F32, name="y_out", bufs=5)
-                src = banks[bank][:].rearrange("m (t p) -> m p t", t=PACK)
-                dst = y_out[b, i // 2][:, i % 2, :].rearrange("m (p t) -> m p t", t=PACK)
-                if eng == "V":
-                    nc.vector.tensor_copy(out=dst, in_=src)
-                else:
-                    nc.scalar.copy(out=dst, in_=src)
-            elif kind == "xcopy":
-                b, e0, e1, eng = op[1:]
-                g, m0, w = blocks[b]
-                if e0 == 0:
-                    y_bf[b] = work.tile([P, GROUP, PACK], BF16, name="y_bf", bufs=2, align_bytes=256)
-                cols = slice(w * e0 // 8, w * e1 // 8)
-                src = y_t[b][:, :, cols].rearrange("p t (a i) -> p a t i", i=4)
-                dst = y_bf[b][:, cols, :].rearrange("p (a i) t -> p a t i", i=4)
-                if eng == "V":
-                    nc.vector.tensor_copy(out=dst, in_=src)
-                else:
-                    nc.scalar.copy(out=dst, in_=src)
-            elif kind == "quanty":
-                b = op[1]
-                g, m0, w = blocks[b]
-                y_codes[b] = work.tile([P, GROUP], U32, name="y_codes", bufs=3, align_bytes=256)
-                nc.vector.quantize_mx(
-                    out=y_codes[b][:, :w].bitcast(FP8X4),
-                    scales=y_scales[4 * g : P, m0 : m0 + w],
-                    in_=y_bf[b][:, :w, :].rearrange("p m t -> p (m t)"),
+                    nc.tensor.transpose(
+                        banks[bank][:, P * t : P * (t + 1)], y_t[b][:, t, P * i : P * (i + 1)], ident[:]
+                    )
+                free.append(bank)
+                if i < on_scalar:
+                    empty_bank(b, i, bank, "scalar")
+            for i0 in range(0, tiles, step):
+                if i0 + step > on_scalar:
+                    empty_bank(b, tiles - 1, bank, "vector")
+                store_y(b, i0, i0 + step)
+
+        def round_y(b, lo, hi, engine):
+            src = y_t[b][:, :, lo:hi]
+            base = BLOCKS[b][1] % GROUP
+            dst = y_bf[:, base + lo : base + hi, :]
+            if engine == "gpsimd":
+                nc.gpsimd.tensor_scalar(
+                    out=dst, in0=src.rearrange("p t m -> p m t"), scalar1=1.0, scalar2=1.0,
+                    op0=ALU.mult, op1=ALU.mult,
                 )
-            elif kind == "storew":
-                b = op[1]
-                g, m0, w = blocks[b]
-                nc.sync.dma_start(out=out_w[g, :, m0 : m0 + w], in_=y_codes[b][:, :w].bitcast(I32))
-            elif kind == "storey":
-                b, i0, i1 = op[1:]
-                g, m0, w = blocks[b]
-                rows = out_0[m0 + P * i0 : m0 + P * i1, GROUP * g : GROUP * (g + 1)]
-                nc.sync.dma_start(out=rows.rearrange("(i m) n -> m i n", m=P), in_=y_out[b, i0 // 2][:, i0 % 2 : i0 % 2 + i1 - i0, :])
-            elif kind == "stores":
-                q = op[1]
+            else:
+                copy_on(
+                    engine, dst.rearrange("p (a i) t -> p a t i", i=4), src.rearrange("p t (a i) -> p a t i", i=4)
+                )
+
+        def quantize_y(b):
+            g, m0, w = BLOCKS[b]
+            if m0 == 0:
+                y_codes[g] = work.tile([P, M], U32, name="y_codes", bufs=2, align_bytes=256)
+            nc.vector.quantize_mx(
+                out=y_codes[g][:, m0 : m0 + w].bitcast(FP8X4),
+                scales=y_scales[4 * g : P, m0 : m0 + w],
+                in_=y_bf[:, m0 % GROUP : m0 % GROUP + w, :].rearrange("p m t -> p (m t)"),
+            )
+            if b >= FINE_STORES_FROM or m0 + w == M:
+                first = m0 if b >= FINE_STORES_FROM else 0
                 nc.sync.dma_start(
-                    out=out_2[:, 4 * q : 4 * q + 4, :].bitcast(I32),
-                    in_=y_scales[32 * q : 32 * q + 16, :].bitcast(I32),
+                    out=out_w[g, :, first : m0 + w], in_=y_codes[g][:, first : m0 + w].bitcast(I32)
                 )
+
+        load_weights(0, 0, 2)
+        load_scales(vol_scales, 0, 1)
+        load_words(0, 1, 0, M)
+        load_weights(1, 0, 1)
+        load_weights(2, 0, 1)
+        load_words(1, 3, 0, GROUP)
+        load_scales(spot_scales, 1, CHUNKS)
+        load_weights(3, 0, 1)
+        load_words(3, CHUNKS, 0, GROUP)
+        load_weights(1, 1, 2)
+        load_words(1, CHUNKS, GROUP, M)
+        load_weights(2, 1, 2)
+        load_weights(3, 1, 2)
+        for c in range(CHUNKS):
+            load_weights(c, 2, GROUPS)
+
+        def interleave_head(k):
+            key, vector_runs = HEAD_CHUNKS[k]
+            interleave(key, "scalar", vector_runs)
+            interleave(key, "vector", vector_runs)
+
+        interleave_head(0)
+        quantize_weights(HEAD_CHUNKS[0][0])
+        interleave_head(1)
+        vega_passes(2 * PACK)
+        interleave_head(2)
+        quantize_weights(HEAD_CHUNKS[1][0])
+        held = [free.pop(0) for t in range(PACK)]
+        for c in DELTA_CHUNKS:
+            quantize_weights((0, c))
+            if c < DELTA_CHUNKS[-1]:
+                interleave_head(c + 2)
+            for t in range(PACK):
+                mx_pass(0, t, c, held[t])
+            if c == DELTA_CHUNKS[0]:
+                vega_passes(PACK)
+        free.extend(held)
+
+        later = list(LATER_CHUNKS)
+        for b in range(len(BLOCKS)):
+            todo = later[: CHUNKS_AFTER_BLOCK[b]] if b < len(CHUNKS_AFTER_BLOCK) else []
+            later = later[len(todo) :]
+            for key in todo:
+                interleave(key, "scalar", VECTOR_RUNS)
+            if b > 0:
+                held = [free.pop(0) for t in range(PACK)]
+                if b in CHUNK_OUTER_BLOCKS:
+                    order = [(t, c) for c in DELTA_CHUNKS for t in range(PACK)]
+                else:
+                    order = [(t, c) for t in range(PACK) for c in DELTA_CHUNKS]
+                for t, c in order:
+                    mx_pass(b, t, c, held[t])
+                free.extend(held)
+                width = BLOCKS[b - 1][2]
+                cut = width - GPSIMD_SCENARIOS[b - 1]
+                round_y(b - 1, cut, width, "gpsimd")
+            for t in range(PACK):
+                add_delta(b, t, held[t])
+            if b > 0:
+                turn_and_store(b - 1)
+            for key in todo:
+                interleave(key, "vector", VECTOR_RUNS)
+            for key in todo[:-1]:
+                quantize_weights(key)
+            if b > 0 and cut > 0:
+                round_y(b - 1, 0, cut, "vector")
+            for key in todo[-1:]:
+                quantize_weights(key)
+            if b > 0:
+                quantize_y(b - 1)
+            if b < LAST:
+                vega_passes(VEGA_AFTER_BLOCK[b])
+
+        width = BLOCKS[LAST][2]
+        round_y(LAST, width // 2, width, "scalar")
+        turn_and_store(LAST)
+        round_y(LAST, 0, width // 2, "vector")
+        quantize_y(LAST)
+        for q in range(QUADRANTS):
+            nc.sync.dma_start(
+                out=out_2[:, 4 * q : 4 * q + 4, :].bitcast(I32),
+                in_=y_scales[32 * q : 32 * q + 16, :].bitcast(I32),
+            )

from contextlib import ExitStack

import concourse.mybir as mybir
from concourse.masks import make_identity

M, KS, KV, N = 1024, 1536, 512, 2048
FLOPS = 2 * M * N * (KS + KV)

F32 = mybir.dt.float32
BF16 = mybir.dt.bfloat16
I32 = mybir.dt.int32
U32 = mybir.dt.uint32
U8 = mybir.dt.uint8
FP8X4 = mybir.dt.float8_e4m3fn_x4
ALU = mybir.AluOpType
ACT = mybir.ActivationFunctionType
ENGINE = mybir.EngineType

P = 128
PACK = 4
GROUP = P * PACK
GROUPS = N // GROUP
CHUNKS = (KV + KS) // GROUP
DELTA_CHUNKS = (1, 2, 3)
QUADRANTS = 4
BANKS = 8

BLOCKS = [(g, m0, GROUP) for g in range(GROUPS) for m0 in (0, GROUP)][:-1] + [
    (GROUPS - 1, GROUP, GROUP // 2),
    (GROUPS - 1, GROUP + GROUP // 2, GROUP // 2),
]
LAST = len(BLOCKS) - 1

RUNS = GROUP // 8
VECTOR_RUNS = 32
HEAD_CHUNKS = (((0, 0), 40), ((1, 0), 40), ((0, 1), RUNS), ((0, 2), RUNS), ((0, 3), 48))
LATER_CHUNKS = [(1, c) for c in DELTA_CHUNKS] + [(g, c) for g in (2, 3) for c in range(CHUNKS)]
CHUNKS_AFTER_BLOCK = (2, 2, 2, 2, 1, 2)
VEGA_AFTER_BLOCK = (2, 2, 4, 4, 0, 4, 4, 4)
CHUNK_OUTER_BLOCKS = (2, 6)
GPSIMD_SCENARIOS = (256, 256, 256, 256, 256, 384, 128, 256)
VECTOR_EMPTIES_LAST_BANK = (5, 7)
FINE_STORES_FROM = 6


def tile_delta_vega_scenario_pnl_g6_kernel(
    tc, spot_words, spot_scales, vol_words, vol_scales, deltas, vegas, vega_weight, carry, quantity,
    out_0, out_1, out_2,
):
    nc = tc.nc

    with ExitStack() as ctx:
        keep = ctx.enter_context(tc.tile_pool(name="keep", bufs=1))
        work = ctx.enter_context(tc.tile_pool(name="work", bufs=1))
        psum = ctx.enter_context(tc.psum_pool(name="psum", bufs=1))
        ctx.enter_context(tc.manual_schedule(engines={ENGINE.PE, ENGINE.SP, ENGINE.Pool, ENGINE.DVE}))

        banks = [psum.tile([P, GROUP], F32, name="bank%d" % i) for i in range(BANKS)]
        ident = keep.tile([P, P], F32)
        a_words = keep.tile([P, CHUNKS, M], U32, align_bytes=256)
        a_scales = keep.tile([P, CHUNKS, M], U8, align_bytes=256)
        y_scales = keep.tile([P, M], U8, align_bytes=256)

        rows = keep.tile([P, GROUP], BF16)
        nc.vector.memset(rows[:].bitcast(I32), 0)
        nc.vector.memset(a_scales[:].rearrange("p c m -> p (c m)").bitcast(I32), 0)
        make_identity(nc, ident[:])
        for k, vector in enumerate((quantity, vega_weight, carry)):
            nc.scalar.dma_start(
                out=rows[GROUPS * k : GROUPS * (k + 1), :], in_=vector.rearrange("(g n) -> g n", g=GROUPS)
            )
        pairs = rows[:].bitcast(F32)
        for u in range(2):
            nc.tensor.transpose(banks[BANKS - 1][:, P * u : P * (u + 1)], pairs[:, u : 2 * P : 2], ident[:])
        vec = keep.tile([P, 3 * GROUPS, PACK], BF16)
        nc.vector.tensor_copy(
            out=vec[:].bitcast(F32),
            in_=banks[BANKS - 1][:, : 2 * P].rearrange("p (u x) -> p x u", u=2)[:, : 3 * GROUPS, :],
        )
        qt, vw, cy = (vec[:, GROUPS * k : GROUPS * (k + 1), :] for k in range(3))
        q32 = keep.tile([P, GROUPS, PACK], F32)
        vwq = keep.tile([P, GROUPS, PACK], F32)
        cq = keep.tile([P, GROUPS, PACK], F32)
        nc.scalar.activation(out=q32[:], in_=qt, func=ACT.Identity)
        nc.vector.tensor_tensor(out=vwq[:], in0=vw, in1=qt, op=ALU.mult)
        nc.vector.tensor_tensor(out=cq[:], in0=cy, in1=qt, op=ALU.mult)

        spot_w = spot_words.rearrange("g p m t -> p g (m t)").bitcast(I32)
        vol_w = vol_words.rearrange("g p m t -> p g (m t)").bitcast(I32)
        out_w = out_1.rearrange("g p m t -> g p (m t)").bitcast(I32)

        raw = {}
        grouped = {}
        w_codes = {}
        w_scales = {}
        y_t = {}
        y_codes = {}
        y_out = {}
        y_bf = keep.tile([P, GROUP, PACK], BF16, align_bytes=256)

        def load_weights(c, g0, g1):
            src = vegas if c == 0 else deltas[GROUP * (c - 1) : GROUP * c, :]
            tile = keep.tile([P, PACK, GROUP * (g1 - g0)], BF16, name="raw%d_%d" % (g0, c))
            nc.sync.dma_start(
                out=tile[:], in_=src[:, GROUP * g0 : GROUP * g1].rearrange("(p j) n -> p j n", j=PACK)
            )
            for g in range(g0, g1):
                raw[g, c] = tile[:, :, GROUP * (g - g0) : GROUP * (g - g0 + 1)]

        def load_words(c0, c1, m0, m1):
            src = vol_w if c0 == 0 else spot_w[:, c0 - 1 : c1 - 1, :]
            nc.sync.dma_start(out=a_words[:, c0:c1, m0:m1].bitcast(I32), in_=src[:, :, m0:m1])

        def load_scales(src, c0, c1):
            for q in range(QUADRANTS):
                nc.sync.dma_start(
                    out=a_scales[32 * q : 32 * q + 4, c0:c1, :].bitcast(I32),
                    in_=src[:, 4 * q : 4 * q + 4, :].rearrange("g r m -> r g m").bitcast(I32),
                )

        def copy_on(engine, dst, src):
            if engine == "vector":
                nc.vector.tensor_copy(out=dst, in_=src)
            else:
                nc.scalar.copy(out=dst, in_=src)

        def interleave(key, engine, vector_runs):
            lo, hi = (0, vector_runs) if engine == "vector" else (vector_runs, RUNS)
            if lo == hi:
                return
            if key == LATER_CHUNKS[CHUNKS_AFTER_BLOCK[0] - 1]:
                grouped[key] = y_bf[:].rearrange("p (t m) j -> p t m j", t=PACK)
            elif key not in grouped:
                grouped[key] = work.tile([P, PACK, P, PACK], BF16, name="grouped", bufs=4, align_bytes=256)
            src = raw[key].rearrange("p j (a b t) -> p a j b t", b=2, t=PACK)[:, lo:hi]
            dst = grouped[key][:].rearrange("p t (a b) j -> p a j b t", b=2)[:, lo:hi]
            copy_on(engine, dst, src)

        def quantize_weights(key):
            name, bufs = ("vega", GROUPS) if key[1] == 0 else ("delta", 7)
            w_codes[key] = work.tile([P, GROUP], U32, name=name + "_codes", bufs=bufs, align_bytes=256)
            w_scales[key] = work.tile([P, GROUP], U8, name=name + "_scales", bufs=bufs, align_bytes=256)
            nc.vector.quantize_mx(
                out=w_codes[key][:].bitcast(FP8X4),
                scales=w_scales[key][:],
                in_=grouped[key][:].rearrange("p t m j -> p (t m j)"),
            )

        def mx_pass(b, t, c, bank):
            g, m0, w = BLOCKS[b]
            nc.tensor.matmul_mx(
                out=banks[bank][:, :w],
                lhsT=w_codes[g, c][:, P * t : P * (t + 1)].bitcast(FP8X4),
                lhsT_scale=w_scales[g, c][:, P * t : P * (t + 1)],
                rhs=a_words[:, c, m0 : m0 + w].bitcast(FP8X4),
                rhs_scale=a_scales[:, c, m0 : m0 + w],
                start=c in (0, DELTA_CHUNKS[0]),
                stop=c in (0, DELTA_CHUNKS[-1]),
            )

        free = list(range(BANKS))
        vega_todo = [(b, t) for b in range(len(BLOCKS)) for t in range(PACK)]

        def vega_passes(count):
            for b, t in vega_todo[:count]:
                g, m0, w = BLOCKS[b]
                bank = free.pop(0)
                mx_pass(b, t, 0, bank)
                if t == 0:
                    name, bufs = ("y_t", 7) if w == GROUP else ("y_t_half", 2)
                    y_t[b] = work.tile([P, PACK, w], F32, name=name, bufs=bufs)
                nc.scalar.activation(
                    out=y_t[b][:, t, :], in_=banks[bank][:, :w], func=ACT.Identity,
                    scale=vwq[:, g, t : t + 1], bias=cq[:, g, t : t + 1],
                )
                free.append(bank)
                vega_todo.remove((b, t))

        def add_delta(b, t, bank):
            g, m0, w = BLOCKS[b]
            nc.vector.scalar_tensor_tensor(
                out=y_t[b][:, t, :], in0=banks[bank][:, :w], scalar=q32[:, g, t : t + 1],
                in1=y_t[b][:, t, :], op0=ALU.mult, op1=ALU.add,
            )

        def empty_bank(b, i, bank, engine):
            if i % 2 == 0:
                y_out[b, i // 2] = work.tile([P, 2, GROUP], F32, name="y_out", bufs=5)
            src = banks[bank][:].rearrange("m (t p) -> m p t", t=PACK)
            dst = y_out[b, i // 2][:, i % 2, :].rearrange("m (p t) -> m p t", t=PACK)
            copy_on(engine, dst, src)

        def store_y(b, i0, i1):
            g, m0, w = BLOCKS[b]
            dst = out_0[m0 + P * i0 : m0 + P * i1, GROUP * g : GROUP * (g + 1)]
            nc.sync.dma_start(
                out=dst.rearrange("(i m) n -> m i n", m=P),
                in_=y_out[b, i0 // 2][:, i0 % 2 : i0 % 2 + i1 - i0, :],
            )

        def turn_and_store(b):
            tiles = BLOCKS[b][2] // P
            on_scalar = tiles - 1 if b in VECTOR_EMPTIES_LAST_BANK else tiles
            step = 1 if b >= FINE_STORES_FROM else 2
            for i in range(tiles):
                bank = free.pop(0)
                for t in range(PACK):
                    nc.tensor.transpose(
                        banks[bank][:, P * t : P * (t + 1)], y_t[b][:, t, P * i : P * (i + 1)], ident[:]
                    )
                free.append(bank)
                if i < on_scalar:
                    empty_bank(b, i, bank, "scalar")
            for i0 in range(0, tiles, step):
                if i0 + step > on_scalar:
                    empty_bank(b, tiles - 1, bank, "vector")
                store_y(b, i0, i0 + step)

        def round_y(b, lo, hi, engine):
            src = y_t[b][:, :, lo:hi]
            base = BLOCKS[b][1] % GROUP
            dst = y_bf[:, base + lo : base + hi, :]
            if engine == "gpsimd":
                nc.gpsimd.tensor_scalar(
                    out=dst, in0=src.rearrange("p t m -> p m t"), scalar1=1.0, scalar2=1.0,
                    op0=ALU.mult, op1=ALU.mult,
                )
            else:
                copy_on(
                    engine, dst.rearrange("p (a i) t -> p a t i", i=4), src.rearrange("p t (a i) -> p a t i", i=4)
                )

        def quantize_y(b):
            g, m0, w = BLOCKS[b]
            if m0 == 0:
                y_codes[g] = work.tile([P, M], U32, name="y_codes", bufs=2, align_bytes=256)
            nc.vector.quantize_mx(
                out=y_codes[g][:, m0 : m0 + w].bitcast(FP8X4),
                scales=y_scales[4 * g : P, m0 : m0 + w],
                in_=y_bf[:, m0 % GROUP : m0 % GROUP + w, :].rearrange("p m t -> p (m t)"),
            )
            if b >= FINE_STORES_FROM or m0 + w == M:
                first = m0 if b >= FINE_STORES_FROM else 0
                nc.sync.dma_start(
                    out=out_w[g, :, first : m0 + w], in_=y_codes[g][:, first : m0 + w].bitcast(I32)
                )

        load_weights(0, 0, 2)
        load_scales(vol_scales, 0, 1)
        load_words(0, 1, 0, M)
        load_weights(1, 0, 1)
        load_weights(2, 0, 1)
        load_words(1, 3, 0, GROUP)
        load_scales(spot_scales, 1, CHUNKS)
        load_weights(3, 0, 1)
        load_words(3, CHUNKS, 0, GROUP)
        load_weights(1, 1, 2)
        load_words(1, CHUNKS, GROUP, M)
        load_weights(2, 1, 2)
        load_weights(3, 1, 2)
        for c in range(CHUNKS):
            load_weights(c, 2, GROUPS)

        def interleave_head(k):
            key, vector_runs = HEAD_CHUNKS[k]
            interleave(key, "scalar", vector_runs)
            interleave(key, "vector", vector_runs)

        interleave_head(0)
        quantize_weights(HEAD_CHUNKS[0][0])
        interleave_head(1)
        vega_passes(2 * PACK)
        interleave_head(2)
        quantize_weights(HEAD_CHUNKS[1][0])
        held = [free.pop(0) for t in range(PACK)]
        for c in DELTA_CHUNKS:
            quantize_weights((0, c))
            if c < DELTA_CHUNKS[-1]:
                interleave_head(c + 2)
            for t in range(PACK):
                mx_pass(0, t, c, held[t])
            if c == DELTA_CHUNKS[0]:
                vega_passes(PACK)
        free.extend(held)

        later = list(LATER_CHUNKS)
        for b in range(len(BLOCKS)):
            todo = later[: CHUNKS_AFTER_BLOCK[b]] if b < len(CHUNKS_AFTER_BLOCK) else []
            later = later[len(todo) :]
            for key in todo:
                interleave(key, "scalar", VECTOR_RUNS)
            if b > 0:
                held = [free.pop(0) for t in range(PACK)]
                if b in CHUNK_OUTER_BLOCKS:
                    order = [(t, c) for c in DELTA_CHUNKS for t in range(PACK)]
                else:
                    order = [(t, c) for t in range(PACK) for c in DELTA_CHUNKS]
                for t, c in order:
                    mx_pass(b, t, c, held[t])
                free.extend(held)
                width = BLOCKS[b - 1][2]
                cut = width - GPSIMD_SCENARIOS[b - 1]
                round_y(b - 1, cut, width, "gpsimd")
            for t in range(PACK):
                add_delta(b, t, held[t])
            if b > 0:
                turn_and_store(b - 1)
            for key in todo:
                interleave(key, "vector", VECTOR_RUNS)
            for key in todo[:-1]:
                quantize_weights(key)
            if b > 0 and cut > 0:
                round_y(b - 1, 0, cut, "vector")
            for key in todo[-1:]:
                quantize_weights(key)
            if b > 0:
                quantize_y(b - 1)
            if b < LAST:
                vega_passes(VEGA_AFTER_BLOCK[b])

        width = BLOCKS[LAST][2]
        round_y(LAST, width // 2, width, "scalar")
        turn_and_store(LAST)
        round_y(LAST, 0, width // 2, "vector")
        quantize_y(LAST)
        for q in range(QUADRANTS):
            nc.sync.dma_start(
                out=out_2[:, 4 * q : 4 * q + 4, :].bitcast(I32),
                in_=y_scales[32 * q : 32 * q + 16, :].bitcast(I32),
            )
